import numpy as np
import ml_dtypes


def mxq(x, axis, fmt="e4m3"):
    dtype, down = {"e4m3": (ml_dtypes.float8_e4m3fn, 7), "e5m2": (ml_dtypes.float8_e5m2, 14)}[fmt]
    v = np.moveaxis(np.asarray(x, np.float32).astype(ml_dtypes.bfloat16).astype(np.float64), axis, -1)
    blocks = v.reshape(v.shape[:-1] + (-1, 32))
    amax = np.abs(blocks).max(-1, keepdims=True)
    byte = np.maximum(np.where(amax > 0, np.frexp(amax)[1] - 1 + 127, 0) - down, 1)
    scale = np.exp2(byte - 127.0)
    codes = (blocks / scale).astype(np.float32).astype(dtype).astype(np.float64)
    return np.moveaxis((codes * scale).reshape(v.shape), -1, axis)


WIDE = False


def mx_kscale(k):
    if not WIDE:
        return np.ones(k)
    levels = np.array([30, -30])
    if k % 512:
        return np.exp2(np.random.permutation(np.resize(levels, k // 32))).repeat(32)
    a = np.empty((k // 512, 16))
    for p in range(k // 512):
        a[p, :8] = np.random.permutation(np.resize(levels, 8))
        for g in range(8):
            far = levels[np.abs(levels - a[p, g]) >= 10]
            a[p, g + 8] = far[np.random.randint(len(far))]
    return np.exp2(a.ravel()).repeat(32)


def f64(x):
    return np.asarray(x).astype(np.float64)


def striped(idx):
    return np.tile(np.asarray(idx).reshape(-1, 16).T, (8, 1)).astype(np.uint16)


def unstriped(offs):
    return offs[:16].T.reshape(-1).astype(np.int64)


def bf(x):
    return np.asarray(x, np.float32).astype(ml_dtypes.bfloat16)


def planes(Y):
    r, m = Y.shape
    b = f64(bf(Y)).reshape(r // 32, 32, m)
    amax = np.abs(b).max(1)
    byte = np.clip(np.where(amax > 0, np.frexp(amax)[1] - 1 + 127 - 7, 1), 1, 254)
    codes = (b * np.exp2(127.0 - byte)[:, None, :]).reshape(r, m).astype(np.float32).astype(ml_dtypes.float8_e4m3fn).view(np.uint8)
    words = codes.reshape(r // 512, 128, 4, m).transpose(0, 1, 3, 2)
    return np.ascontiguousarray(words), np.ascontiguousarray(byte.astype(np.uint8).reshape(r // 512, 16, m))


T, K, N, J = 1024, 512, 1024, 512


def setup_inputs():
    n = np.random.standard_normal
    idx = np.random.permutation(N)[:J]
    ft = mx_kscale(T)
    return {
        "xt": (n((T, K)) * ft[:, None]).astype(np.float32),
        "g": (n((T, N)) * np.exp(0.5 * n((T, 1))) / ft[:, None]).astype(np.float32),
        "mom": (1.0 * n((K, N))).astype(np.float32),
        "sec": (np.random.uniform(0.2, 2.0, (K, N))).astype(np.float32),
        "offs": striped(idx),
    }


def reference(xt, g, mom, sec, offs):
    idx = unstriped(offs)
    xtq = mxq(f64(xt), 0, "e4m3")
    gidxq = mxq(f64(g)[:, idx], 0, "e5m2")
    w = xtq.T @ gidxq
    y = (0.03 * w + 0.9 * f64(mom)[:, idx]) / (np.sqrt(f64(sec)[:, idx]) + 0.1)
    words, scales = planes(y)
    return y, words, scales

@@ -1,0 +1,147 @@
+from contextlib import ExitStack
+
+import concourse.mybir as mybir
+
+T, K, N, J = 1024, 512, 1024, 512
+FLOPS = 2 * T * K * J
+
+F32 = mybir.dt.float32
+BF16 = mybir.dt.bfloat16
+I32 = mybir.dt.int32
+U32 = mybir.dt.uint32
+U16 = mybir.dt.uint16
+U8 = mybir.dt.uint8
+E4M3 = mybir.dt.float8_e4m3fn_x4
+E5M2 = mybir.dt.float8_e5m2_x4
+ACT = mybir.ActivationFunctionType
+ALU = mybir.AluOpType
+
+P = 128
+PACK = 4
+PASS = P * PACK
+PASSES = T // PASS
+
+
+def tile_list_sparse_scaled_step_pl_kernel(tc, xt, g, mom, sec, offs, out_0, out_1, out_2):
+    nc = tc.nc
+    with ExitStack() as ctx:
+        keep = ctx.enter_context(tc.tile_pool(name="keep", bufs=1))
+        psum = ctx.enter_context(tc.psum_pool(name="psum", bufs=1))
+
+        def sb(shape, dtype, name):
+            return keep.tile(shape, dtype, name=name, align_bytes=64)
+
+        offsets = keep.tile([P, J // 16], U16, name="offsets")
+        nc.sync.dma_start(offsets[:], offs)
+
+        def load_rows(src, row, name):
+            rows = sb([P, N], F32, name)
+            nc.sync.dma_start(out=rows[:], in_=src.rearrange("(p r) n -> p r n", r=PACK)[:, row, :])
+            return rows
+
+        g_rows = [[load_rows(g[a * PASS : (a + 1) * PASS, :], r, f"g_{a}_{r}") for r in range(PACK)] for a in range(PASSES)]
+        x_raw = []
+        for a in range(PASSES):
+            raw = sb([P, PACK, K], F32, f"x_raw_{a}")
+            nc.sync.dma_start(out=raw[:], in_=xt[a * PASS : (a + 1) * PASS, :].rearrange("(p r) k -> p r k", r=PACK))
+            x_raw.append(raw)
+        sec_rows = [load_rows(sec, r, f"sec_{r}") for r in range(PACK)]
+        mom_rows = [load_rows(mom, r, f"mom_{r}") for r in range(PACK)]
+
+        one = sb([P, 1], F32, "one")
+        nc.gpsimd.memset(one[:], 1.0)
+        shift = sb([P, 1], F32, "shift")
+        nc.scalar.activation(shift[:], one[:], ACT.Ln, scale=1.0 / 160.0)
+
+        def quantize(grouped, dtype, name):
+            codes = sb([P, PASS], U32, name + "_codes")
+            scales = sb([P, PASS], U8, name + "_scales")
+            nc.vector.quantize_mx(out=codes[:].bitcast(dtype), scales=scales[:], in_=grouped[:])
+            return codes, scales
+
+        def gather_g(a):
+            picked = sb([P, PACK, J], F32, f"g_picked_{a}")
+            for r in range(PACK):
+                nc.vector.tensor_copy(picked[:, r, :], g_rows[a][r][:].indirect(offsets[:]))
+            grouped = sb([P, J * PACK], BF16, f"g_grouped_{a}")
+            nc.scalar.copy(
+                grouped[:].rearrange("p (c i r) -> p c r i", i=4, r=PACK),
+                picked[:].rearrange("p r (c i) -> p c r i", i=4),
+            )
+            return grouped
+
+        def group_x(a, copy):
+            grouped = sb([P, K * PACK], BF16, f"x_grouped_{a}")
+            copy(
+                grouped[:].rearrange("p (s m r) -> p m r s", s=PACK, r=PACK),
+                x_raw[a][:].rearrange("p r (m s) -> p m r s", s=PACK),
+            )
+            return grouped
+
+        acc = [psum.tile([P, J], F32, name=f"acc_{s}") for s in range(PACK)]
+
+        def multiply(a, x_q, g_q):
+            for s in range(PACK):
+                cols = slice(s * P, (s + 1) * P)
+                nc.tensor.matmul_mx(
+                    out=acc[s][:],
+                    lhsT=x_q[0][:, cols].bitcast(E4M3),
+                    lhsT_scale=x_q[1][:, cols],
+                    rhs=g_q[0][:].bitcast(E5M2),
+                    rhs_scale=g_q[1][:],
+                    start=(a == 0),
+                    stop=(a == PASSES - 1),
+                )
+
+        g_grouped = [gather_g(a) for a in range(PASSES)]
+        g_q0 = quantize(g_grouped[0], E5M2, "g0")
+        x_grouped0 = group_x(0, nc.vector.tensor_copy)
+        g_q1 = quantize(g_grouped[1], E5M2, "g1")
+        x_q0 = quantize(x_grouped0, E4M3, "x0")
+        multiply(0, x_q0, g_q0)
+        x_grouped1 = group_x(1, nc.scalar.copy)
+
+        sec_picked = sb([P, PACK, J], F32, "sec_picked")
+        sec_log = sb([P, PACK, J], F32, "sec_log")
+        w_part = sb([P, PACK, J], F32, "w_part")
+        mixed = sb([P, PACK, J], F32, "mixed")
+        y = sb([P, PACK, J], F32, "y")
+        y_grouped = sb([P, J * PACK], BF16, "y_grouped")
+
+        def gather_sec(s):
+            nc.vector.tensor_copy(sec_picked[:, s, :], sec_rows[s][:].indirect(offsets[:]))
+            nc.scalar.activation(sec_log[:, s, :], sec_picked[:, s, :], ACT.Ln, scale=2.0**-8, bias=2.0**-63)
+
+        gather_sec(0)
+        gather_sec(1)
+        x_q1 = quantize(x_grouped1, E4M3, "x1")
+        multiply(1, x_q1, g_q1)
+        gather_sec(2)
+        for s in range(PACK):
+            nc.scalar.activation(w_part[:, s, :], acc[s][:], ACT.Copy, scale=1.0 / 30.0)
+        gather_sec(3)
+        damp = [sec_picked[:, (s + 2) % PACK, :] for s in range(PACK)]
+        for h in range(2):
+            nc.scalar.activation(sec_picked[:, 2 - 2 * h : 4 - 2 * h, :], sec_log[:, 2 * h : 2 * h + 2, :], ACT.Sigmoid, scale=-0.5, bias=shift[:])
+        for s in range(PACK):
+            nc.vector.tensor_tensor(mixed[:, s, :], mom_rows[s][:].indirect(offsets[:]), w_part[:, s, :], ALU.add)
+
+        def group_y(h, copy):
+            rows = slice(2 * h, 2 * h + 2)
+            copy(
+                y_grouped[:].rearrange("p (c i r) -> p c r i", i=4, r=PACK)[:, :, rows, :],
+                y[:].rearrange("p r (c i) -> p c r i", i=4)[:, :, rows, :],
+            )
+
+        out_rows = out_0.rearrange("(p r) j -> p r j", r=PACK)
+        for s in range(PACK):
+            nc.vector.scalar_tensor_tensor(y[:, s, :], mixed[:, s, :], 9.0, damp[s], ALU.mult, ALU.mult)
+            nc.sync.dma_start(out=out_rows[:, s, :], in_=y[:, s, :])
+            if s == 1:
+                group_y(0, nc.scalar.copy)
+        group_y(1, nc.vector.tensor_copy)
+        y_codes, y_scales = quantize(y_grouped, E4M3, "y")
+        nc.sync.dma_start(out=out_1[0].rearrange("p c r -> p (c r)").bitcast(I32), in_=y_codes[:].bitcast(I32))
+        for q in range(4):
+            queue = nc.scalar if q % 2 else nc.sync
+            queue.dma_start(out=out_2[0, 4 * q : 4 * q + 4, :].bitcast(I32), in_=y_scales[32 * q : 32 * q + 4, :].bitcast(I32))

@@ -20,26 +20,31 @@ P = 128
 PACK = 4
 PASS = P * PACK
 PASSES = T // PASS
+HALF = J // 2
 
 
 def tile_list_sparse_scaled_step_pl_kernel(tc, xt, g, mom, sec, offs, out_0, out_1, out_2):
     nc = tc.nc
     with ExitStack() as ctx:
+        lists = ctx.enter_context(tc.tile_pool(name="lists", bufs=1))
         keep = ctx.enter_context(tc.tile_pool(name="keep", bufs=1))
         psum = ctx.enter_context(tc.psum_pool(name="psum", bufs=1))
 
-        def sb(shape, dtype, name):
-            return keep.tile(shape, dtype, name=name, align_bytes=64)
-
-        offsets = keep.tile([P, J // 16], U16, name="offsets")
-        nc.sync.dma_start(offsets[:], offs)
+        def sb(shape, dtype, name, tag=None):
+            return keep.tile(shape, dtype, name=name, tag=tag or name, align_bytes=64)
 
         def load_rows(src, row, name):
             rows = sb([P, N], F32, name)
             nc.sync.dma_start(out=rows[:], in_=src.rearrange("(p r) n -> p r n", r=PACK)[:, row, :])
             return rows
 
-        g_rows = [[load_rows(g[a * PASS : (a + 1) * PASS, :], r, f"g_{a}_{r}") for r in range(PACK)] for a in range(PASSES)]
+        offsets = lists.tile([P, J // 16], U16, name="offsets")
+        g_rows = []
+        for i in range(PASSES * PACK):
+            a, r = divmod(i, PACK)
+            g_rows.append(load_rows(g[a * PASS : (a + 1) * PASS, :], r, f"g_{a}_{r}"))
+            if i == 0:
+                nc.sync.dma_start(offsets[:], offs)
         x_raw = []
         for a in range(PASSES):
             raw = sb([P, PACK, K], F32, f"x_raw_{a}")
@@ -53,30 +58,37 @@ def tile_list_sparse_scaled_step_pl_kernel(tc, xt, g, mom, sec, offs, out_0, out
         shift = sb([P, 1], F32, "shift")
         nc.scalar.activation(shift[:], one[:], ACT.Ln, scale=1.0 / 160.0)
 
-        def quantize(grouped, dtype, name):
-            codes = sb([P, PASS], U32, name + "_codes")
+        damp_first = sb([P, 2, J], F32, "damp_first")
+        floor, zero = damp_first[:, 0, 0:1], damp_first[:, 0, 1:2]
+        nc.gpsimd.memset(floor, 2.0**-63)
+        nc.gpsimd.memset(zero, 0.0)
+
+        g_grouped = []
+        for a in range(PASSES):
+            picked = sb([P, PACK, J], F32, f"g_picked_{a}")
+            for r in range(PACK):
+                nc.vector.tensor_copy(picked[:, r, :], g_rows[a * PACK + r][:].indirect(offsets[:]))
+            grouped = sb([P, J * PACK], BF16, f"g_grouped_{a}")
+            for rows in [slice(0, 4)] if a == 0 else [slice(0, 2), slice(2, 4)]:
+                nc.scalar.copy(
+                    grouped[:].rearrange("p (c i r) -> p c r i", i=4, r=PACK)[:, :, rows, :],
+                    picked[:].rearrange("p r (c i) -> p c r i", i=4)[:, :, rows, :],
+                )
+            g_grouped.append(grouped)
+
+        def quantize(grouped, dtype, name, tag=None):
+            codes = sb([P, PASS], U32, name + "_codes", tag=tag)
             scales = sb([P, PASS], U8, name + "_scales")
             nc.vector.quantize_mx(out=codes[:].bitcast(dtype), scales=scales[:], in_=grouped[:])
             return codes, scales
 
-        def gather_g(a):
-            picked = sb([P, PACK, J], F32, f"g_picked_{a}")
-            for r in range(PACK):
-                nc.vector.tensor_copy(picked[:, r, :], g_rows[a][r][:].indirect(offsets[:]))
-            grouped = sb([P, J * PACK], BF16, f"g_grouped_{a}")
-            nc.scalar.copy(
-                grouped[:].rearrange("p (c i r) -> p c r i", i=4, r=PACK),
-                picked[:].rearrange("p r (c i) -> p c r i", i=4),
-            )
-            return grouped
+        x_grouped = [sb([P, K * PACK], BF16, f"x_grouped_{a}") for a in range(PASSES)]
 
-        def group_x(a, copy):
-            grouped = sb([P, K * PACK], BF16, f"x_grouped_{a}")
+        def group_x(a, m0, m1, copy):
             copy(
-                grouped[:].rearrange("p (s m r) -> p m r s", s=PACK, r=PACK),
-                x_raw[a][:].rearrange("p r (m s) -> p m r s", s=PACK),
+                x_grouped[a][:].rearrange("p (u v m r) -> p u m r v", u=2, v=2, r=PACK)[:, :, m0:m1],
+                x_raw[a][:].rearrange("p r (m u v) -> p u m r v", u=2, v=2)[:, :, m0:m1],
             )
-            return grouped
 
         acc = [psum.tile([P, J], F32, name=f"acc_{s}") for s in range(PACK)]
 
@@ -93,55 +105,79 @@ def tile_list_sparse_scaled_step_pl_kernel(tc, xt, g, mom, sec, offs, out_0, out
                     stop=(a == PASSES - 1),
                 )
 
-        g_grouped = [gather_g(a) for a in range(PASSES)]
-        g_q0 = quantize(g_grouped[0], E5M2, "g0")
-        x_grouped0 = group_x(0, nc.vector.tensor_copy)
-        g_q1 = quantize(g_grouped[1], E5M2, "g1")
-        x_q0 = quantize(x_grouped0, E4M3, "x0")
-        multiply(0, x_q0, g_q0)
-        x_grouped1 = group_x(1, nc.scalar.copy)
-
-        sec_picked = sb([P, PACK, J], F32, "sec_picked")
         sec_log = sb([P, PACK, J], F32, "sec_log")
-        w_part = sb([P, PACK, J], F32, "w_part")
-        mixed = sb([P, PACK, J], F32, "mixed")
-        y = sb([P, PACK, J], F32, "y")
-        y_grouped = sb([P, J * PACK], BF16, "y_grouped")
 
         def gather_sec(s):
-            nc.vector.tensor_copy(sec_picked[:, s, :], sec_rows[s][:].indirect(offsets[:]))
-            nc.scalar.activation(sec_log[:, s, :], sec_picked[:, s, :], ACT.Ln, scale=2.0**-8, bias=2.0**-63)
+            picked = sb([P, J], F32, f"sec_picked_{s}", tag="x_grouped_0" if s == 0 else None)
+            nc.vector.tensor_copy(picked[:], sec_rows[s][:].indirect(offsets[:]))
+            nc.scalar.activation(sec_log[:, s, :], picked[:], ACT.Ln, scale=2.0**-8, bias=floor)
 
+        group_x(0, 0, P, nc.vector.tensor_copy)
+        g_q0 = quantize(g_grouped[0], E5M2, "g0", tag="x_raw_0")
+        group_x(1, 0, P, nc.scalar.copy)
+        multiply(0, quantize(x_grouped[0], E4M3, "x0"), g_q0)
+        g_q1 = quantize(g_grouped[1], E5M2, "g1", tag="g_grouped_0")
         gather_sec(0)
-        gather_sec(1)
-        x_q1 = quantize(x_grouped1, E4M3, "x1")
-        multiply(1, x_q1, g_q1)
-        gather_sec(2)
+        multiply(1, quantize(x_grouped[1], E4M3, "x1", tag="sec_0"), g_q1)
+        w_part = sb([P, PACK, J], F32, "w_part")
         for s in range(PACK):
-            nc.scalar.activation(w_part[:, s, :], acc[s][:], ACT.Copy, scale=1.0 / 30.0)
-        gather_sec(3)
-        damp = [sec_picked[:, (s + 2) % PACK, :] for s in range(PACK)]
-        for h in range(2):
-            nc.scalar.activation(sec_picked[:, 2 - 2 * h : 4 - 2 * h, :], sec_log[:, 2 * h : 2 * h + 2, :], ACT.Sigmoid, scale=-0.5, bias=shift[:])
-        for s in range(PACK):
-            nc.vector.tensor_tensor(mixed[:, s, :], mom_rows[s][:].indirect(offsets[:]), w_part[:, s, :], ALU.add)
+            nc.scalar.activation(w_part[:, s, :], acc[s][:], ACT.Identity, scale=1.0 / 30.0, bias=zero)
+        for s in range(1, PACK):
+            gather_sec(s)
+        nc.scalar.activation(damp_first[:], sec_log[:, 0:2, :], ACT.Sigmoid, scale=-0.5, bias=shift[:])
+        nc.scalar.activation(sec_log[:, 0:2, :], sec_log[:, 2:4, :], ACT.Sigmoid, scale=-0.5, bias=shift[:])
+        damp = [damp_first[:, 0, :], damp_first[:, 1, :], sec_log[:, 0, :], sec_log[:, 1, :]]
 
-        def group_y(h, copy):
+        mixed = sb([P, PACK, J], F32, "mixed")
+
+        def mixed_part(s, c0, c1):
+            return mixed[:, 2, 0:HALF] if (s, c0) == (3, HALF) else mixed[:, s, c0:c1]
+
+        def mix(s, c0, c1):
+            nc.vector.tensor_tensor(mixed_part(s, c0, c1), mom_rows[s][:].indirect(offsets[:, c0 // 16 : c1 // 16]), w_part[:, s, c0:c1], ALU.add)
+
+        for s in range(PACK - 1):
+            mix(s, 0, J)
+        y = sb([P, PACK, J], F32, "y", tag="mom_2")
+        y_grouped = sb([P, J * PACK], BF16, "y_grouped")
+        y_codes = sb([P, J], U32, "y_codes")
+        y_scales = sb([P, J], U8, "y_scales")
+        out_rows = out_0.rearrange("(p r) j -> p r j", r=PACK)
+
+        def finish(s, c0, c1):
+            nc.vector.scalar_tensor_tensor(y[:, s, c0:c1], mixed_part(s, c0, c1), 9.0, damp[s][:, c0:c1], ALU.mult, ALU.mult)
+
+        def group_y(h, c0, c1, copy):
             rows = slice(2 * h, 2 * h + 2)
             copy(
-                y_grouped[:].rearrange("p (c i r) -> p c r i", i=4, r=PACK)[:, :, rows, :],
-                y[:].rearrange("p r (c i) -> p c r i", i=4)[:, :, rows, :],
+                y_grouped[:].rearrange("p (c i r) -> p c r i", i=4, r=PACK)[:, c0 // 4 : c1 // 4, rows, :],
+                y[:].rearrange("p r (c i) -> p c r i", i=4)[:, c0 // 4 : c1 // 4, rows, :],
             )
 
-        out_rows = out_0.rearrange("(p r) j -> p r j", r=PACK)
-        for s in range(PACK):
-            nc.vector.scalar_tensor_tensor(y[:, s, :], mixed[:, s, :], 9.0, damp[s], ALU.mult, ALU.mult)
+        words = out_1[0].rearrange("p c r -> p (c r)").bitcast(I32)
+
+        def store(s):
             nc.sync.dma_start(out=out_rows[:, s, :], in_=y[:, s, :])
-            if s == 1:
-                group_y(0, nc.scalar.copy)
-        group_y(1, nc.vector.tensor_copy)
-        y_codes, y_scales = quantize(y_grouped, E4M3, "y")
-        nc.sync.dma_start(out=out_1[0].rearrange("p c r -> p (c r)").bitcast(I32), in_=y_codes[:].bitcast(I32))
+
+        def hand_on(c0, c1):
+            nc.vector.quantize_mx(out=y_codes[:, c0:c1].bitcast(E4M3), scales=y_scales[:, c0:c1], in_=y_grouped[:, PACK * c0 : PACK * c1])
+            nc.sync.dma_start(out=words[:, c0:c1], in_=y_codes[:, c0:c1].bitcast(I32))
+
+        for s in range(2):
+            finish(s, 0, J)
+            store(s)
+        group_y(0, 0, J, nc.scalar.copy)
+        mix(3, 0, HALF)
+        finish(2, 0, J)
+        store(2)
+        finish(3, 0, HALF)
+        group_y(1, 0, HALF, nc.scalar.copy)
+        mix(3, HALF, J)
+        finish(3, HALF, J)
+        store(3)
+        hand_on(0, HALF)
+        group_y(1, HALF, J, nc.vector.tensor_copy)
+        hand_on(HALF, J)
         for q in range(4):
             queue = nc.scalar if q % 2 else nc.sync
             queue.dma_start(out=out_2[0, 4 * q : 4 * q + 4, :].bitcast(I32), in_=y_scales[32 * q : 32 * q + 4, :].bitcast(I32))

@@ -112,72 +112,78 @@ def tile_list_sparse_scaled_step_pl_kernel(tc, xt, g, mom, sec, offs, out_0, out
             nc.vector.tensor_copy(picked[:], sec_rows[s][:].indirect(offsets[:]))
             nc.scalar.activation(sec_log[:, s, :], picked[:], ACT.Ln, scale=2.0**-8, bias=floor)
 
+        g_q0 = quantize(g_grouped[0], E5M2, "g0", tag="g_1_3")
         group_x(0, 0, P, nc.vector.tensor_copy)
-        g_q0 = quantize(g_grouped[0], E5M2, "g0", tag="x_raw_0")
         group_x(1, 0, P, nc.scalar.copy)
+        g_q1 = quantize(g_grouped[1], E5M2, "g1", tag="x_raw_0")
         multiply(0, quantize(x_grouped[0], E4M3, "x0"), g_q0)
-        g_q1 = quantize(g_grouped[1], E5M2, "g1", tag="g_grouped_0")
         gather_sec(0)
-        multiply(1, quantize(x_grouped[1], E4M3, "x1", tag="sec_0"), g_q1)
-        w_part = sb([P, PACK, J], F32, "w_part")
+        multiply(1, quantize(x_grouped[1], E4M3, "x1"), g_q1)
+        w_low = sb([P, PACK - 1, J], F32, "w_low")
+        shared = sb([P, HALF + 2 * J], F32, "shared")
+        w_part = [w_low[:, s, :] for s in range(PACK - 1)] + [shared[:, 0:J]]
         for s in range(PACK):
-            nc.scalar.activation(w_part[:, s, :], acc[s][:], ACT.Identity, scale=1.0 / 30.0, bias=zero)
+            nc.scalar.activation(w_part[s], acc[s][:], ACT.Identity, scale=1.0 / 30.0, bias=zero)
         for s in range(1, PACK):
             gather_sec(s)
         nc.scalar.activation(damp_first[:], sec_log[:, 0:2, :], ACT.Sigmoid, scale=-0.5, bias=shift[:])
         nc.scalar.activation(sec_log[:, 0:2, :], sec_log[:, 2:4, :], ACT.Sigmoid, scale=-0.5, bias=shift[:])
         damp = [damp_first[:, 0, :], damp_first[:, 1, :], sec_log[:, 0, :], sec_log[:, 1, :]]
 
+        last = PACK - 1
+        early, late = slice(HALF, J), slice(0, HALF)
+        whole = slice(0, J)
         mixed = sb([P, PACK, J], F32, "mixed")
-
-        def mixed_part(s, c0, c1):
-            return mixed[:, 2, 0:HALF] if (s, c0) == (3, HALF) else mixed[:, s, c0:c1]
-
-        def mix(s, c0, c1):
-            nc.vector.tensor_tensor(mixed_part(s, c0, c1), mom_rows[s][:].indirect(offsets[:, c0 // 16 : c1 // 16]), w_part[:, s, c0:c1], ALU.add)
-
-        for s in range(PACK - 1):
-            mix(s, 0, J)
-        y = sb([P, PACK, J], F32, "y", tag="mom_2")
+        y_high = sb([P, 2, J], F32, "y_high")
+        y_pairs = [shared[:, HALF:].rearrange("p (r j) -> p r j", r=2), y_high[:]]
         y_grouped = sb([P, J * PACK], BF16, "y_grouped")
         y_codes = sb([P, J], U32, "y_codes")
         y_scales = sb([P, J], U8, "y_scales")
         out_rows = out_0.rearrange("(p r) j -> p r j", r=PACK)
-
-        def finish(s, c0, c1):
-            nc.vector.scalar_tensor_tensor(y[:, s, c0:c1], mixed_part(s, c0, c1), 9.0, damp[s][:, c0:c1], ALU.mult, ALU.mult)
-
-        def group_y(h, c0, c1, copy):
-            rows = slice(2 * h, 2 * h + 2)
-            copy(
-                y_grouped[:].rearrange("p (c i r) -> p c r i", i=4, r=PACK)[:, c0 // 4 : c1 // 4, rows, :],
-                y[:].rearrange("p r (c i) -> p c r i", i=4)[:, c0 // 4 : c1 // 4, rows, :],
-            )
-
         words = out_1[0].rearrange("p c r -> p (c r)").bitcast(I32)
 
+        def mixed_part(s, cols):
+            return mixed[:, s, cols]
+
+        def mix(s, cols):
+            listed = offsets[:, cols.start // 16 : cols.stop // 16]
+            nc.vector.tensor_tensor(mixed_part(s, cols), mom_rows[s][:].indirect(listed), w_part[s][:, cols], ALU.add)
+
+        def finish(s, cols):
+            nc.vector.scalar_tensor_tensor(y_pairs[s // 2][:, s % 2, cols], mixed_part(s, cols), 9.0, damp[s][:, cols], ALU.mult, ALU.mult)
+
         def store(s):
-            nc.sync.dma_start(out=out_rows[:, s, :], in_=y[:, s, :])
+            nc.sync.dma_start(out=out_rows[:, s, :], in_=y_pairs[s // 2][:, s % 2, :])
 
-        def hand_on(c0, c1):
-            nc.vector.quantize_mx(out=y_codes[:, c0:c1].bitcast(E4M3), scales=y_scales[:, c0:c1], in_=y_grouped[:, PACK * c0 : PACK * c1])
-            nc.sync.dma_start(out=words[:, c0:c1], in_=y_codes[:, c0:c1].bitcast(I32))
+        def group_y(h, cols, copy):
+            quads = slice(cols.start // 4, cols.stop // 4)
+            copy(
+                y_grouped[:].rearrange("p (c i r) -> p c r i", i=4, r=PACK)[:, quads, 2 * h : 2 * h + 2, :],
+                y_pairs[h].rearrange("p r (c i) -> p c r i", i=4)[:, quads],
+            )
 
-        for s in range(2):
-            finish(s, 0, J)
+        def hand_on(cols):
+            nc.vector.quantize_mx(
+                out=y_codes[:, cols].bitcast(E4M3), scales=y_scales[:, cols], in_=y_grouped[:, PACK * cols.start : PACK * cols.stop]
+            )
+            nc.sync.dma_start(out=words[:, cols], in_=y_codes[:, cols].bitcast(I32))
+
+        for s in range(last):
+            mix(s, whole)
+        halves = (early, late)
+        for cols in halves:
+            mix(last, cols)
+        for s in range(PACK):
+            for cols in halves if s == last else [whole]:
+                finish(s, cols)
             store(s)
-        group_y(0, 0, J, nc.scalar.copy)
-        mix(3, 0, HALF)
-        finish(2, 0, J)
-        store(2)
-        finish(3, 0, HALF)
-        group_y(1, 0, HALF, nc.scalar.copy)
-        mix(3, HALF, J)
-        finish(3, HALF, J)
-        store(3)
-        hand_on(0, HALF)
-        group_y(1, HALF, J, nc.vector.tensor_copy)
-        hand_on(HALF, J)
+            if s == 1:
+                for cols in halves:
+                    group_y(0, cols, nc.scalar.copy)
+        for cols in halves:
+            group_y(1, cols, nc.vector.tensor_copy)
+        for cols in halves:
+            hand_on(cols)
         for q in range(4):
             queue = nc.scalar if q % 2 else nc.sync
             queue.dma_start(out=out_2[0, 4 * q : 4 * q + 4, :].bitcast(I32), in_=y_scales[32 * q : 32 * q + 4, :].bitcast(I32))

from contextlib import ExitStack

import concourse.mybir as mybir

T, K, N, J = 1024, 512, 1024, 512
FLOPS = 2 * T * K * J

F32 = mybir.dt.float32
BF16 = mybir.dt.bfloat16
I32 = mybir.dt.int32
U32 = mybir.dt.uint32
U16 = mybir.dt.uint16
U8 = mybir.dt.uint8
E4M3 = mybir.dt.float8_e4m3fn_x4
E5M2 = mybir.dt.float8_e5m2_x4
ACT = mybir.ActivationFunctionType
ALU = mybir.AluOpType

P = 128
PACK = 4
PASS = P * PACK
PASSES = T // PASS
HALF = J // 2


def tile_list_sparse_scaled_step_pl_kernel(tc, xt, g, mom, sec, offs, out_0, out_1, out_2):
    nc = tc.nc
    with ExitStack() as ctx:
        lists = ctx.enter_context(tc.tile_pool(name="lists", bufs=1))
        keep = ctx.enter_context(tc.tile_pool(name="keep", bufs=1))
        psum = ctx.enter_context(tc.psum_pool(name="psum", bufs=1))

        def sb(shape, dtype, name, tag=None):
            return keep.tile(shape, dtype, name=name, tag=tag or name, align_bytes=64)

        def load_rows(src, row, name):
            rows = sb([P, N], F32, name)
            nc.sync.dma_start(out=rows[:], in_=src.rearrange("(p r) n -> p r n", r=PACK)[:, row, :])
            return rows

        offsets = lists.tile([P, J // 16], U16, name="offsets")
        g_rows = []
        for i in range(PASSES * PACK):
            a, r = divmod(i, PACK)
            g_rows.append(load_rows(g[a * PASS : (a + 1) * PASS, :], r, f"g_{a}_{r}"))
            if i == 0:
                nc.sync.dma_start(offsets[:], offs)
        x_raw = []
        for a in range(PASSES):
            raw = sb([P, PACK, K], F32, f"x_raw_{a}")
            nc.sync.dma_start(out=raw[:], in_=xt[a * PASS : (a + 1) * PASS, :].rearrange("(p r) k -> p r k", r=PACK))
            x_raw.append(raw)
        sec_rows = [load_rows(sec, r, f"sec_{r}") for r in range(PACK)]
        mom_rows = [load_rows(mom, r, f"mom_{r}") for r in range(PACK)]

        one = sb([P, 1], F32, "one")
        nc.gpsimd.memset(one[:], 1.0)
        shift = sb([P, 1], F32, "shift")
        nc.scalar.activation(shift[:], one[:], ACT.Ln, scale=1.0 / 160.0)

        damp_first = sb([P, 2, J], F32, "damp_first")
        floor, zero = damp_first[:, 0, 0:1], damp_first[:, 0, 1:2]
        nc.gpsimd.memset(floor, 2.0**-63)
        nc.gpsimd.memset(zero, 0.0)

        g_grouped = []
        for a in range(PASSES):
            picked = sb([P, PACK, J], F32, f"g_picked_{a}")
            for r in range(PACK):
                nc.vector.tensor_copy(picked[:, r, :], g_rows[a * PACK + r][:].indirect(offsets[:]))
            grouped = sb([P, J * PACK], BF16, f"g_grouped_{a}")
            for rows in [slice(0, 4)] if a == 0 else [slice(0, 2), slice(2, 4)]:
                nc.scalar.copy(
                    grouped[:].rearrange("p (c i r) -> p c r i", i=4, r=PACK)[:, :, rows, :],
                    picked[:].rearrange("p r (c i) -> p c r i", i=4)[:, :, rows, :],
                )
            g_grouped.append(grouped)

        def quantize(grouped, dtype, name, tag=None):
            codes = sb([P, PASS], U32, name + "_codes", tag=tag)
            scales = sb([P, PASS], U8, name + "_scales")
            nc.vector.quantize_mx(out=codes[:].bitcast(dtype), scales=scales[:], in_=grouped[:])
            return codes, scales

        x_grouped = [sb([P, K * PACK], BF16, f"x_grouped_{a}") for a in range(PASSES)]

        def group_x(a, m0, m1, copy):
            copy(
                x_grouped[a][:].rearrange("p (u v m r) -> p u m r v", u=2, v=2, r=PACK)[:, :, m0:m1],
                x_raw[a][:].rearrange("p r (m u v) -> p u m r v", u=2, v=2)[:, :, m0:m1],
            )

        acc = [psum.tile([P, J], F32, name=f"acc_{s}") for s in range(PACK)]

        def multiply(a, x_q, g_q):
            for s in range(PACK):
                cols = slice(s * P, (s + 1) * P)
                nc.tensor.matmul_mx(
                    out=acc[s][:],
                    lhsT=x_q[0][:, cols].bitcast(E4M3),
                    lhsT_scale=x_q[1][:, cols],
                    rhs=g_q[0][:].bitcast(E5M2),
                    rhs_scale=g_q[1][:],
                    start=(a == 0),
                    stop=(a == PASSES - 1),
                )

        sec_log = sb([P, PACK, J], F32, "sec_log")

        def gather_sec(s):
            picked = sb([P, J], F32, f"sec_picked_{s}", tag="x_grouped_0" if s == 0 else None)
            nc.vector.tensor_copy(picked[:], sec_rows[s][:].indirect(offsets[:]))
            nc.scalar.activation(sec_log[:, s, :], picked[:], ACT.Ln, scale=2.0**-8, bias=floor)

        g_q0 = quantize(g_grouped[0], E5M2, "g0", tag="g_1_3")
        group_x(0, 0, P, nc.vector.tensor_copy)
        group_x(1, 0, P, nc.scalar.copy)
        g_q1 = quantize(g_grouped[1], E5M2, "g1", tag="x_raw_0")
        multiply(0, quantize(x_grouped[0], E4M3, "x0"), g_q0)
        gather_sec(0)
        multiply(1, quantize(x_grouped[1], E4M3, "x1"), g_q1)
        w_low = sb([P, PACK - 1, J], F32, "w_low")
        shared = sb([P, HALF + 2 * J], F32, "shared")
        w_part = [w_low[:, s, :] for s in range(PACK - 1)] + [shared[:, 0:J]]
        for s in range(PACK):
            nc.scalar.activation(w_part[s], acc[s][:], ACT.Identity, scale=1.0 / 30.0, bias=zero)
        for s in range(1, PACK):
            gather_sec(s)
        nc.scalar.activation(damp_first[:], sec_log[:, 0:2, :], ACT.Sigmoid, scale=-0.5, bias=shift[:])
        nc.scalar.activation(sec_log[:, 0:2, :], sec_log[:, 2:4, :], ACT.Sigmoid, scale=-0.5, bias=shift[:])
        damp = [damp_first[:, 0, :], damp_first[:, 1, :], sec_log[:, 0, :], sec_log[:, 1, :]]

        last = PACK - 1
        early, late = slice(HALF, J), slice(0, HALF)
        whole = slice(0, J)
        mixed = sb([P, PACK, J], F32, "mixed")
        y_high = sb([P, 2, J], F32, "y_high")
        y_pairs = [shared[:, HALF:].rearrange("p (r j) -> p r j", r=2), y_high[:]]
        y_grouped = sb([P, J * PACK], BF16, "y_grouped")
        y_codes = sb([P, J], U32, "y_codes")
        y_scales = sb([P, J], U8, "y_scales")
        out_rows = out_0.rearrange("(p r) j -> p r j", r=PACK)
        words = out_1[0].rearrange("p c r -> p (c r)").bitcast(I32)

        def mixed_part(s, cols):
            return mixed[:, s, cols]

        def mix(s, cols):
            listed = offsets[:, cols.start // 16 : cols.stop // 16]
            nc.vector.tensor_tensor(mixed_part(s, cols), mom_rows[s][:].indirect(listed), w_part[s][:, cols], ALU.add)

        def finish(s, cols):
            nc.vector.scalar_tensor_tensor(y_pairs[s // 2][:, s % 2, cols], mixed_part(s, cols), 9.0, damp[s][:, cols], ALU.mult, ALU.mult)

        def store(s):
            nc.sync.dma_start(out=out_rows[:, s, :], in_=y_pairs[s // 2][:, s % 2, :])

        def group_y(h, cols, copy):
            quads = slice(cols.start // 4, cols.stop // 4)
            copy(
                y_grouped[:].rearrange("p (c i r) -> p c r i", i=4, r=PACK)[:, quads, 2 * h : 2 * h + 2, :],
                y_pairs[h].rearrange("p r (c i) -> p c r i", i=4)[:, quads],
            )

        def hand_on(cols):
            nc.vector.quantize_mx(
                out=y_codes[:, cols].bitcast(E4M3), scales=y_scales[:, cols], in_=y_grouped[:, PACK * cols.start : PACK * cols.stop]
            )
            nc.sync.dma_start(out=words[:, cols], in_=y_codes[:, cols].bitcast(I32))

        for s in range(last):
            mix(s, whole)
        halves = (early, late)
        for cols in halves:
            mix(last, cols)
        for s in range(PACK):
            for cols in halves if s == last else [whole]:
                finish(s, cols)
            store(s)
            if s == 1:
                for cols in halves:
                    group_y(0, cols, nc.scalar.copy)
        for cols in halves:
            group_y(1, cols, nc.vector.tensor_copy)
        for cols in halves:
            hand_on(cols)
        for q in range(4):
            queue = nc.scalar if q % 2 else nc.sync
            queue.dma_start(out=out_2[0, 4 * q : 4 * q + 4, :].bitcast(I32), in_=y_scales[32 * q : 32 * q + 4, :].bitcast(I32))
